import numpy as np, ml_dtypes
CORES = [113,118,241,246]
N = 4
TK = 64
def setup_inputs(rng):
    x = rng.standard_normal((N, 128, TK), dtype=np.float32).astype(ml_dtypes.bfloat16); w1 = (rng.standard_normal((N, 128, 128), dtype=np.float32) / 8).astype(ml_dtypes.bfloat16)
    wa = np.concatenate(list(w1.astype(np.float64)), axis=1)
    for r in range(N):
        while True:
            near = (np.abs(wa.T @ x[r].astype(np.float64)) < 2e-4).any(axis=0)
            if not near.any(): break
            x[r][:, near] = rng.standard_normal((128, int(near.sum())), dtype=np.float32).astype(ml_dtypes.bfloat16)
    return {"x": x, "dy": rng.standard_normal((N, 128, TK), dtype=np.float32).astype(ml_dtypes.bfloat16), "w1": w1, "w2t": (rng.standard_normal((N, 128, 128), dtype=np.float32) / 8).astype(ml_dtypes.bfloat16)}
def setup_inputs_big(rng):
    d = setup_inputs(rng)
    for k in ("x", "dy", "w1", "w2t"): d[k] = (d[k].astype(np.float32) * 1024.0).astype(d[k].dtype)
    return d
def setup_inputs_small(rng):
    d = setup_inputs(rng)
    for k in ("x", "dy", "w1", "w2t"): d[k] = (d[k].astype(np.float32) * (1 / 1024.0)).astype(d[k].dtype)
    return d
def setup_inputs_apart(rng):
    d = setup_inputs(rng)
    f = (10.0 ** rng.permutation(np.linspace(-1.5, 1.5, N))).astype(np.float32).reshape(N, 1, 1)
    for k in ("x", "dy", "w1", "w2t"): d[k] = (d[k].astype(np.float32) * f).astype(d[k].dtype)
    return d
def reference(x, dy, w1, w2t):
    X, DY, W1, W2T = x.astype(np.float64), dy.astype(np.float64), w1.astype(np.float64), w2t.astype(np.float64)
    dx = np.zeros((N, 128, TK))
    for r in range(N):
        for j in range(N):
            dx[r] += W1[j] @ ((W1[j].T @ X[r] > 0) * (W2T[j].T @ DY[r]))
    return {"dx": dx.astype(ml_dtypes.bfloat16)}

from concourse.bass import DstId, RemoteDMATransfer
from concourse.mybir import AluOpType

N = 4
TK = 64
D = 128
WS = 2 * D

SCRATCH = {
    "w": ("sbuf", [128, N * WS], "bfloat16"),
    "xd": ("sbuf", [128, 2 * TK], "bfloat16"),
    "ones": ("sbuf", [128, D], "bfloat16"),
    "ident": ("sbuf", [128, D], "bfloat16"),
    "wt": ("sbuf", [128, N * D], "bfloat16"),
    "m": ("sbuf", [128, N * TK], "bfloat16"),
    "gg": ("sbuf", [128, N * TK], "bfloat16"),
    "o": ("sbuf", [128, TK], "bfloat16"),
    "tp0": ("psum", [128, 1024], "bfloat16"), "tp1": ("psum", [128, 1024], "bfloat16"),
    "zp0": ("psum", [128, 512], "float32"), "zp1": ("psum", [128, 512], "float32"),
    "up0": ("psum", [128, 512], "float32"), "up1": ("psum", [128, 512], "float32"),
    "acc": ("psum", [128, 512], "float32"),
}
SEMAPHORES = (["wl", "xl", "one", "idn", "sent", "dacc", "oc", "stored"]
              + ["arr%d" % j for j in range(N)]
              + ["%s%d" % (k, j) for k in ("tT", "tZ", "tU", "v") for j in range(N)])


def _bits(mask):
    return bin(mask).count("1")


def _same_chip(topo, a, b):
    return topo.host(a) == topo.host(b) and topo.chip(a) == topo.chip(b)


def _common(topo, src, dsts):
    masks = [topo.mask(src, d) for d in dsts]
    m = masks[0]
    for k in masks[1:]:
        m &= k
    return m


def _plan(topo, cores, src):
    others = [d for d in cores if d != src]
    near = [d for d in others if _same_chip(topo, src, d)]
    far = [d for d in others if not _same_chip(topo, src, d)]
    far.sort(key=lambda d: topo.die(d) != topo.die(src))
    far_mask = _common(topo, src, far)
    near_mask = _common(topo, src, near) & ~far_mask
    return far, far_mask, near, near_mask


def rank_program(g, core, T, topo):
    rank = T.rank_of(core)
    if rank is None:
        return
    S = T.sem
    cores = list(T.cores)
    slot = lambda j: T.w[:, j * WS:(j + 1) * WS]

    g.sync.dma_start(T.w[:, rank * WS:rank * WS + D], T.w1[:, :]).then_inc(S.wl, 16)
    g.scalar.dma_start(T.w[:, rank * WS + D:(rank + 1) * WS], T.w2t[:, :]).then_inc(S.wl, 16)
    g.sync.dma_start(T.xd[:, 0:TK], T.x[:, :]).then_inc(S.xl, 16)
    g.scalar.dma_start(T.xd[:, TK:2 * TK], T.dy[:, :]).then_inc(S.xl, 16)

    g.vector.memset(T.ones[:, :], 1.0).then_inc(S.one, 1)
    g.wait_ge(S.one, 1)
    g.affine_select(T.ident[:, :], T.ones[:, :], [[-1, D]], AluOpType.is_equal, 0.0, 0, 1).then_inc(S.idn, 1)

    far, far_mask, near, near_mask = _plan(topo, cores, core)
    ids = lambda ds: [DstId(rid=topo.addr(d, core)[0], pnc=topo.addr(d, core)[1]) for d in ds]
    arr = S["arr%d" % rank]
    g.wait_ge(S.wl, 32)
    g.remote_dma_fused([
        RemoteDMATransfer(dst_ids=ids(far), dma_engine_mask=far_mask, remote_sem=arr,
                          srcs=[slot(rank)], dsts=[slot(rank) for _ in far]),
        RemoteDMATransfer(dst_ids=ids(near), dma_engine_mask=near_mask, remote_sem=arr,
                          srcs=[slot(rank)], dsts=[slot(rank) for _ in near]),
    ], local_sem=S.sent)

    order = [core] + near + far

    def landed(src):
        f, fm, n, nm = _plan(topo, cores, src)
        return _bits(fm) if core in f else _bits(nm)

    te, ve = g.tensor, g.vector
    x, dy = T.xd[:, 0:TK], T.xd[:, TK:2 * TK]

    def front(k):
        j = T.rank_of(order[k])
        b = k % 2
        if k == 0:
            te.wait_ge(S.wl, 32)
            te.wait_ge(S.idn, 1)
        else:
            te.wait_ge(S["arr%d" % j], landed(order[k]))
        te.transpose(T["tp%d" % b][:, 0:D], T.w[:, j * WS:j * WS + D], T.ident[:, :]).then_inc(S["tT%d" % j], 1)
        if k == 0:
            te.wait_ge(S.xl, 32)
        te.matmul(T["zp%d" % b][:, 0:TK], T.w[:, j * WS:j * WS + D], x, True, True).then_inc(S["tZ%d" % j], 1)
        te.matmul(T["up%d" % b][:, 0:TK], T.w[:, j * WS + D:(j + 1) * WS], dy, True, True).then_inc(S["tU%d" % j], 1)
        v = S["v%d" % j]
        ve.wait_ge(S["tT%d" % j], 1)
        ve.tensor_copy(T.wt[:, j * D:(j + 1) * D], T["tp%d" % b][:, 0:D]).then_inc(v, 1)
        ve.wait_ge(S["tZ%d" % j], 1)
        ve.tensor_scalar(T.m[:, j * TK:(j + 1) * TK], T["zp%d" % b][:, 0:TK], 0.0, None, AluOpType.is_gt).then_inc(v, 1)
        ve.wait_ge(S["tU%d" % j], 1)
        ve.wait_ge(v, 2)
        ve.tensor_tensor(T.gg[:, j * TK:(j + 1) * TK], T.m[:, j * TK:(j + 1) * TK], T["up%d" % b][:, 0:TK],
                         AluOpType.mult).then_inc(v, 1)

    def back(k):
        j = T.rank_of(order[k])
        te.wait_ge(S["v%d" % j], 3)
        i = te.matmul(T.acc[:, 0:TK], T.wt[:, j * D:(j + 1) * D], T.gg[:, j * TK:(j + 1) * TK], k == 0, k == N - 1)
        if k == N - 1:
            i.then_inc(S.dacc, 1)

    front(0); back(0)
    front(1); back(1)
    front(2); front(3); back(2); back(3)

    ve.wait_ge(S.dacc, 1)
    ve.tensor_copy(T.o[:, :], T.acc[:, 0:TK]).then_inc(S.oc, 1)
    g.sync.wait_ge(S.oc, 1)
    g.sync.dma_start(T.dx[:, :], T.o[:, :]).then_inc(S.stored, 16)
    g.sync.wait_ge(S.stored, 16)
    g.wait_ge(S.sent, _bits(far_mask) + _bits(near_mask))
